import numpy as np
import ml_dtypes


def mxq(x, axis, fmt="e4m3"):
    dtype, down = {"e4m3": (ml_dtypes.float8_e4m3fn, 7), "e5m2": (ml_dtypes.float8_e5m2, 14)}[fmt]
    v = np.moveaxis(np.asarray(x, np.float32).astype(ml_dtypes.bfloat16).astype(np.float64), axis, -1)
    blocks = v.reshape(v.shape[:-1] + (-1, 32))
    amax = np.abs(blocks).max(-1, keepdims=True)
    byte = np.maximum(np.where(amax > 0, np.frexp(amax)[1] - 1 + 127, 0) - down, 1)
    scale = np.exp2(byte - 127.0)
    codes = (blocks / scale).astype(np.float32).astype(dtype).astype(np.float64)
    return np.moveaxis((codes * scale).reshape(v.shape), -1, axis)


WIDE = False


def mx_kscale(k):
    if not WIDE:
        return np.ones(k)
    levels = np.array([10, -10, 5, -5, 0])
    if k % 512:
        return np.exp2(np.random.permutation(np.resize(levels, k // 32))).repeat(32)
    a = np.empty((k // 512, 16))
    for p in range(k // 512):
        a[p, :8] = np.random.permutation(np.resize(levels, 8))
        for g in range(8):
            far = levels[np.abs(levels - a[p, g]) >= 10]
            a[p, g + 8] = far[np.random.randint(len(far))]
    return np.exp2(a.ravel()).repeat(32)


def f64(x):
    return np.asarray(x).astype(np.float64)


def striped(idx):
    return np.tile(idx.reshape(-1, 16).T, (8, 1)).astype(np.uint16)


def unstriped(offs):
    return offs[:16].T.reshape(-1).astype(np.int64)


E2M1 = np.array([0.0, 0.5, 1.0, 1.5, 2.0, 3.0, 4.0, 6.0, -0.0, -0.5, -1.0, -1.5, -2.0, -3.0, -4.0, -6.0])


def pack_weight(w, fmt):
    k, n = w.shape
    w = f64(np.asarray(w, np.float32).astype(ml_dtypes.bfloat16)).reshape(k // 32, 32, n)
    amax = np.abs(w).max(1)
    if fmt == "e4m3":
        byte = np.frexp(amax)[1] - 1 + 127 - 7
    else:
        mant, ex = np.frexp(amax / 6.0)
        byte = np.where(mant > 0.5, ex, ex - 1) + 127
    byte = np.clip(np.where(amax > 0, byte, 1), 1, 254)
    scaled = (w * np.exp2(127.0 - byte)[:, None, :]).reshape(k, n).astype(np.float32)
    by_word = np.ascontiguousarray(scaled.reshape(k // 512, 128, 4, n).transpose(0, 1, 3, 2))
    if fmt == "e4m3":
        words = by_word.astype(ml_dtypes.float8_e4m3fn).view(np.uint8)
    else:
        c = by_word.astype(ml_dtypes.float4_e2m1fn).view(np.uint8) & 0xF
        words = (c[..., 0::2] | (c[..., 1::2] << 4)).reshape(k // 512, 128, 2 * n)
    return np.ascontiguousarray(words), np.ascontiguousarray(byte.astype(np.uint8).reshape(k // 512, 16, n))


def unpack_weight(words, scales, fmt):
    g, _, n = scales.shape
    words = np.ascontiguousarray(words).reshape(g, 128, n, -1)
    if fmt == "e4m3":
        vals = words.view(ml_dtypes.float8_e4m3fn).astype(np.float64)
    else:
        nib = np.empty((g, 128, n, 4), np.uint8)
        nib[..., 0::2] = words & 0xF
        nib[..., 1::2] = words >> 4
        vals = E2M1[nib]
    vals = vals * np.repeat(np.exp2(scales.astype(np.float64) - 127.0), 8, axis=1)[..., None]
    return vals.transpose(0, 1, 3, 2).reshape(g * 512, n)


def relu(v):
    return np.maximum(v, 0.0)


K, T, E, C, H, N = 1536, 1024, 8, 256, 512, 128


def by_expert(wq, xq):
    return np.concatenate([wq[e].T @ xq[:, e * C:(e + 1) * C] for e in range(E)], axis=1)


def setup_inputs():
    n = np.random.standard_normal
    s = mx_kscale(K)[:, None]
    u = mx_kscale(H)
    first = np.random.permutation(np.repeat(np.arange(E), T // E))
    second = (first + 1 + np.random.permutation(np.repeat(np.arange(E - 1), -(-T // (E - 1)))[:T])) % E
    while np.bincount(second, minlength=E).max() != T // E:
        load = np.bincount(second, minlength=E); hi, lo = int(load.argmax()), int(load.argmin())
        t = np.flatnonzero((second == hi) & (first != lo))[0]; second[t] = lo
    slot_token = np.empty(E * C, np.int64); pos = np.empty((2, T), np.int64); fill = np.zeros(E, np.int64)
    place = np.stack([np.random.permutation(C) for _ in range(E)])
    for r, deal in enumerate((first, second)):
        for t in np.random.permutation(T):
            e = deal[t]; j = e * C + place[e, fill[e]]; fill[e] += 1; slot_token[j] = t; pos[r, t] = j
    g = np.random.uniform(0.2, 0.8, T)
    w1 = [pack_weight(m, "e2m1") for m in n((E, K, H)) / np.sqrt(K) / s[None] * u[None, None, :]]
    w2 = [pack_weight(m, "e2m1") for m in n((E, H, N)) / np.sqrt(H) / u[None, :, None]]
    x = pack_weight(n((K, T)) * s, "e4m3")
    return {
        "x_words": x[0],
        "x_scales": x[1],
        "w1_words": np.stack([m[0] for m in w1]),
        "w1_scales": np.stack([m[1] for m in w1]),
        "w2_words": np.stack([m[0] for m in w2]),
        "w2_scales": np.stack([m[1] for m in w2]),
        "gate": np.stack([np.tile(g, (N, 1)), np.tile(1.0 - g, (N, 1))]).astype(np.float32),
        "offs": striped(slot_token),
        "pos1": striped(pos[0]),
        "pos2": striped(pos[1]),
    }


def reference(x_words, x_scales, w1_words, w1_scales, w2_words, w2_scales, gate, offs, pos1, pos2):
    idx = unstriped(offs)
    w1 = np.stack([unpack_weight(w1_words[e], w1_scales[e], "e2m1") for e in range(E)])
    w2 = np.stack([unpack_weight(w2_words[e], w2_scales[e], "e2m1") for e in range(E)])
    xq = unpack_weight(x_words, x_scales, "e4m3")[:, idx]
    h = relu(by_expert(w1, xq))
    y = by_expert(w2, mxq(h, 0, "e4m3"))
    return f64(gate[0]) * y[:, unstriped(pos1)] + f64(gate[1]) * y[:, unstriped(pos2)]

@@ -1,0 +1,248 @@
+from contextlib import ExitStack
+
+import concourse.mybir as mybir
+from concourse.masks import make_identity
+
+K, T, E, C, H, N = 1536, 1024, 8, 256, 512, 128
+FLOPS = 2 * E * C * (K * H + H * N)
+
+F32 = mybir.dt.float32
+BF16 = mybir.dt.bfloat16
+I32 = mybir.dt.int32
+U32 = mybir.dt.uint32
+U16 = mybir.dt.uint16
+U8 = mybir.dt.uint8
+FP8X4 = mybir.dt.float8_e4m3fn_x4
+FP4X4 = mybir.dt.float4_e2m1fn_x4
+ACT = mybir.ActivationFunctionType
+ALU = mybir.AluOpType
+
+P = 128
+PASSES = K // 512
+SLOTS = E * C
+SHIFT_ROWS = 112
+SCALE_CHUNKS = ((0, 2), (2, 5), (5, 8))
+W1_SCALE_CHUNKS = ((0, 1), (1, 3), (3, 8))
+OUT_CHUNKS = ((0, 512), (512, 768), (768, 1024))
+
+
+def tile_moe_pkd_mlp_relu_kernel(
+    tc, x_words, x_scales, w1_words, w1_scales, w2_words, w2_scales, gate, offs, pos1, pos2, out
+):
+    nc = tc.nc
+    with ExitStack() as ctx:
+        keep = ctx.enter_context(tc.tile_pool(name="keep", bufs=1))
+        ring = ctx.enter_context(tc.tile_pool(name="ring", bufs=3))
+        psum = ctx.enter_context(tc.psum_pool(name="psum", bufs=1))
+
+        offs_t = keep.tile([P, SLOTS // 16], U16, name="offs_t")
+        pos_t = [keep.tile([P, T // 16], U16, name=f"pos_t{j}") for j in range(2)]
+        xw = [keep.tile([P, T], I32, name=f"xw{a}", align_bytes=64) for a in range(PASSES)]
+        xs = keep.tile([P, T], U8, name="xs", align_bytes=64)
+        shifted = {a: keep.tile([P, SLOTS], U8, name=f"shifted{a}", align_bytes=64) for a in (1, 2)}
+        gw = {}
+        gs = {}
+        w1w = [keep.tile([P, PASSES, 2 * H], U8, name=f"w1w{e}", align_bytes=64) for e in range(E)]
+        w1s = keep.tile([P, E * PASSES, H], U8, name="w1s", align_bytes=64)
+        w2w = keep.tile([P, E, 2 * N], U8, name="w2w", align_bytes=64)
+        w2s = keep.tile([P, E, N], U8, name="w2s", align_bytes=64)
+        gate_t = [keep.tile([P, T], F32, name=f"gate_t{j}") for j in range(2)]
+        y = keep.tile([P, SLOTS], F32, name="y")
+        ident = keep.tile([P, P], F32, name="ident")
+        warm = keep.tile([P, 8], F32, name="warm")
+
+        def load_w1_scales(queue, chunk):
+            e0, e1 = W1_SCALE_CHUNKS[chunk]
+            rows = w1_scales[e0:e1].rearrange("e s q i -> q (e s) i")
+            for q in range(4):
+                queue.dma_start(
+                    out=w1s[32 * q : 32 * q + 4, e0 * PASSES : e1 * PASSES, :].bitcast(I32),
+                    in_=rows[4 * q : 4 * q + 4].bitcast(I32),
+                )
+
+        def load_w1(e):
+            nc.sync.dma_start(out=w1w[e][:].bitcast(I32), in_=w1_words[e].rearrange("s p c -> p s c").bitcast(I32))
+
+        def load_x_words(a):
+            nc.sync.dma_start(out=xw[a][:], in_=x_words[a].rearrange("p t r -> p (t r)").bitcast(I32))
+
+        def load_x_scales(queue, q):
+            queue.dma_start(
+                out=xs[32 * q : 32 * q + 4 * PASSES, :].bitcast(I32),
+                in_=x_scales[:, 4 * q : 4 * q + 4, :].bitcast(I32),
+            )
+
+        def gather_scales(chunk, queue):
+            e0, e1 = SCALE_CHUNKS[chunk]
+            width = (e1 - e0) * C
+            packed = ring.tile([P, 3 * C], U8, name="packed", bufs=2, align_bytes=64)
+            nc.vector.tensor_copy(packed[:, 0:width], xs[:].indirect(offs_t[:, e0 * C // 16 : e1 * C // 16]))
+            for e in range(e0, e1):
+                gs[e] = packed[:, (e - e0) * C : (e - e0 + 1) * C]
+            for a in (1, 2):
+                queue.dma_start(
+                    out=shifted[a][0:SHIFT_ROWS, e0 * C : e1 * C].bitcast(I32),
+                    in_=packed[4 * a : 4 * a + SHIFT_ROWS, 0:width].bitcast(I32),
+                )
+
+        def gather_words(a, s0, s1):
+            e = s0 // C
+            if (e, a) not in gw:
+                gw[e, a] = ring.tile([P, C], U32, name=f"gw{a}", bufs=2, align_bytes=64)
+            nc.vector.tensor_copy(
+                gw[e, a][:, s0 - e * C : s1 - e * C], xw[a][:].bitcast(U32).indirect(offs_t[:, s0 // 16 : s1 // 16])
+            )
+
+        def bank(index):
+            return psum.tile([P, H], F32, name=f"bank{index % 8}")
+
+        hidden = {}
+        grouped = {}
+
+        def first_layer(tile_index):
+            e = tile_index * P // C
+            cols = slice(tile_index * P, (tile_index + 1) * P)
+            own = slice(tile_index * P - e * C, (tile_index + 1) * P - e * C)
+            acc = bank(tile_index)
+            for a in range(PASSES):
+                nc.tensor.matmul_mx(
+                    out=acc[:],
+                    lhsT=gw[e, a][:, own].bitcast(FP8X4),
+                    lhsT_scale=gs[e][:, own] if a == 0 else shifted[a][:, cols],
+                    rhs=w1w[e][:, a, :].bitcast(FP4X4),
+                    rhs_scale=w1s[:, e * PASSES + a, :],
+                    start=(a == 0),
+                    stop=(a == PASSES - 1),
+                )
+            h = ring.tile([P, H], BF16, name="h", bufs=6, align_bytes=64)
+            nc.scalar.activation(
+                h[:].rearrange("s (u p d) -> s u p d", u=2, d=2),
+                acc[:].rearrange("s (p u d) -> s u p d", u=2, d=2),
+                ACT.Relu,
+            )
+            hidden[tile_index] = h
+
+        def turn(t0, t1, bank_index):
+            tiles = t1 - t0
+            turned = bank(bank_index)[:].rearrange("p (j u s) -> p j u s", j=2, u=2)
+            for j in range(tiles):
+                words = hidden[t0 + j][:].bitcast(F32)
+                for u in range(2):
+                    nc.tensor.transpose(turned[:, j, u, :], words[:, u * P : (u + 1) * P], ident[:])
+            g = ring.tile([P, 2, P, 2], F32, name="g", bufs=4, align_bytes=64)
+            nc.scalar.copy(g[:, 0:tiles], turned[:, 0:tiles].rearrange("p j u s -> p j s u"))
+            grouped[t0] = g
+
+        def second_layer(t0, t1, bank_index):
+            width = (t1 - t0) * P
+            e = t0 * P // C
+            codes = ring.tile([P, C], U32, name="codes", align_bytes=64)
+            scales = ring.tile([P, C], U8, name="scales", align_bytes=64)
+            values = grouped[t0][:].rearrange("p j s u -> p (j s u)").bitcast(BF16)
+            nc.vector.quantize_mx(
+                out=codes[:, 0:width].bitcast(FP8X4), scales=scales[:, 0:width], in_=values[:, 0 : 4 * width]
+            )
+            acc_y = bank(bank_index)
+            nc.tensor.matmul_mx(
+                out=acc_y[:, 0:width],
+                lhsT=w2w[:, e, :].bitcast(FP4X4),
+                lhsT_scale=w2s[:, e, :],
+                rhs=codes[:, 0:width].bitcast(FP8X4),
+                rhs_scale=scales[:, 0:width],
+                start=True,
+                stop=True,
+            )
+            nc.scalar.copy(y[:, t0 * P : t1 * P], acc_y[:, 0:width])
+
+        nc.vector.memset(xs[:].bitcast(I32), 0)
+        nc.sync.dma_start(offs_t[:], offs)
+        load_x_words(0)
+        for q in range(4):
+            load_x_scales(nc.sync if q < 2 else nc.scalar, q)
+        load_x_words(1)
+        load_x_words(2)
+        for e0, e1 in W1_SCALE_CHUNKS[:1]:
+            nc.vector.memset(w1s[:, e0 * PASSES : e1 * PASSES, :].bitcast(I32), 0)
+        for a in (1, 2):
+            nc.vector.memset(shifted[a][:].bitcast(I32), 0)
+        for e0, e1 in W1_SCALE_CHUNKS[1:]:
+            nc.vector.memset(w1s[:, e0 * PASSES : e1 * PASSES, :].bitcast(I32), 0)
+        nc.vector.memset(w2s[:].bitcast(I32), 0)
+        load_w1(0)
+        load_w1_scales(nc.scalar, 0)
+        make_identity(nc, ident[:])
+        nc.scalar.activation(warm[:], ident[:, 0:8], ACT.Relu)
+
+        gather_words(0, 0, C)
+        gather_scales(0, nc.scalar)
+        gather_words(0, C, 2 * C)
+        gather_words(1, 0, C)
+        gather_words(2, 0, C)
+        load_w1_scales(nc.sync, 1)
+        load_w1(1)
+        nc.sync.dma_start(out=w2w[:].bitcast(I32), in_=w2_words.rearrange("e o p c -> p (e o) c").bitcast(I32))
+        w2_rows = w2_scales.rearrange("e o q n -> q (e o) n")
+        for q in range(4):
+            nc.sync.dma_start(out=w2s[32 * q : 32 * q + 4].bitcast(I32), in_=w2_rows[4 * q : 4 * q + 4].bitcast(I32))
+        load_w1(2)
+
+        for e in range(E):
+            for tile_index in (2 * e, 2 * e + 1):
+                first_layer(tile_index)
+            if e >= 1:
+                turn(2 * e - 2, 2 * e, 2 * e)
+            if e >= 3:
+                second_layer(2 * e - 6, 2 * e - 4, 2 * e + 1)
+            nxt = e + 1
+            if nxt < E - 1:
+                for a in range(PASSES):
+                    if (nxt, a) != (1, 0):
+                        gather_words(a, nxt * C, (nxt + 1) * C)
+            elif nxt == E - 1:
+                for half in range(2):
+                    for a in range(PASSES):
+                        gather_words(a, nxt * C + half * P, nxt * C + (half + 1) * P)
+            if e == 0:
+                gather_scales(1, nc.sync)
+                load_w1_scales(nc.sync, 2)
+                load_w1(3)
+                load_w1(4)
+            if e == 2:
+                gather_scales(2, nc.sync)
+                for later in (5, 6, 7):
+                    load_w1(later)
+                nc.sync.dma_start(pos_t[0][:], pos1)
+                nc.sync.dma_start(pos_t[1][:], pos2)
+                for j in range(2):
+                    nc.sync.dma_start(out=gate_t[j][:], in_=gate[j])
+        last = 2 * E
+        second_layer(last - 6, last - 4, last)
+        turn(last - 2, last - 1, last + 1)
+        turn(last - 1, last, last + 2)
+        second_layer(last - 4, last - 2, last + 3)
+        second_layer(last - 2, last - 1, last + 4)
+        second_layer(last - 1, last, last + 5)
+
+        terms = []
+        for t0, t1 in OUT_CHUNKS:
+            pair = [keep.tile([P, t1 - t0], F32, name=f"term{j}_{t0}") for j in range(2)]
+            terms.append(pair)
+
+        def fetch(chunk, j):
+            t0, t1 = OUT_CHUNKS[chunk]
+            nc.vector.tensor_tensor(
+                terms[chunk][j][:], y[:].indirect(pos_t[j][:, t0 // 16 : t1 // 16]), gate_t[j][:, t0:t1], ALU.mult
+            )
+
+        def finish(chunk):
+            t0, t1 = OUT_CHUNKS[chunk]
+            total = keep.tile([P, t1 - t0], F32, name=f"total{t0}")
+            nc.vector.tensor_tensor(total[:], terms[chunk][0][:], terms[chunk][1][:], ALU.add)
+            nc.sync.dma_start(out=out[:, t0:t1], in_=total[:])
+
+        for chunk in range(len(OUT_CHUNKS)):
+            fetch(chunk, 0)
+            if chunk > 0:
+                finish(chunk - 1)
+            fetch(chunk, 1)
+        finish(len(OUT_CHUNKS) - 1)

@@ -21,8 +21,8 @@ P = 128
 PASSES = K // 512
 SLOTS = E * C
 SHIFT_ROWS = 112
-SCALE_CHUNKS = ((0, 2), (2, 5), (5, 8))
-W1_SCALE_CHUNKS = ((0, 1), (1, 3), (3, 8))
+SCALE_CHUNKS = ((0, 1), (1, 3), (3, 5), (5, 8))
+W1_SCALE_CHUNKS = ((0, 1), (1, 4), (4, 8))
 OUT_CHUNKS = ((0, 512), (512, 768), (768, 1024))
 
 
@@ -42,11 +42,11 @@ def tile_moe_pkd_mlp_relu_kernel(
         shifted = {a: keep.tile([P, SLOTS], U8, name=f"shifted{a}", align_bytes=64) for a in (1, 2)}
         gw = {}
         gs = {}
-        w1w = [keep.tile([P, PASSES, 2 * H], U8, name=f"w1w{e}", align_bytes=64) for e in range(E)]
+        w1w = {}
         w1s = keep.tile([P, E * PASSES, H], U8, name="w1s", align_bytes=64)
         w2w = keep.tile([P, E, 2 * N], U8, name="w2w", align_bytes=64)
         w2s = keep.tile([P, E, N], U8, name="w2s", align_bytes=64)
-        gate_t = [keep.tile([P, T], F32, name=f"gate_t{j}") for j in range(2)]
+        gate_t = {}
         y = keep.tile([P, SLOTS], F32, name="y")
         ident = keep.tile([P, P], F32, name="ident")
         warm = keep.tile([P, 8], F32, name="warm")
@@ -60,7 +60,12 @@ def tile_moe_pkd_mlp_relu_kernel(
                     in_=rows[4 * q : 4 * q + 4].bitcast(I32),
                 )
 
+        def load_gate(j):
+            gate_t[j] = ring.tile([P, T], F32, name=f"gate_t{j}", tag="stream", bufs=3, align_bytes=64)
+            nc.sync.dma_start(out=gate_t[j][:], in_=gate[j])
+
         def load_w1(e):
+            w1w[e] = ring.tile([P, PASSES, 2 * H], U8, name=f"w1w{e}", tag="stream", bufs=3, align_bytes=64)
             nc.sync.dma_start(out=w1w[e][:].bitcast(I32), in_=w1_words[e].rearrange("s p c -> p s c").bitcast(I32))
 
         def load_x_words(a):
@@ -122,18 +127,18 @@ def tile_moe_pkd_mlp_relu_kernel(
             )
             hidden[tile_index] = h
 
-        def turn(t0, t1, bank_index):
+        def turn(t0, t1, bank_index, copy):
             tiles = t1 - t0
             turned = bank(bank_index)[:].rearrange("p (j u s) -> p j u s", j=2, u=2)
             for j in range(tiles):
                 words = hidden[t0 + j][:].bitcast(F32)
                 for u in range(2):
                     nc.tensor.transpose(turned[:, j, u, :], words[:, u * P : (u + 1) * P], ident[:])
-            g = ring.tile([P, 2, P, 2], F32, name="g", bufs=4, align_bytes=64)
-            nc.scalar.copy(g[:, 0:tiles], turned[:, 0:tiles].rearrange("p j u s -> p j s u"))
+            g = ring.tile([P, 2, P, 2], F32, name="g", bufs=5, align_bytes=64)
+            copy(g[:, 0:tiles], turned[:, 0:tiles].rearrange("p j u s -> p j s u"))
             grouped[t0] = g
 
-        def second_layer(t0, t1, bank_index):
+        def second_layer(t0, t1, bank_index, copy):
             width = (t1 - t0) * P
             e = t0 * P // C
             codes = ring.tile([P, C], U32, name="codes", align_bytes=64)
@@ -152,13 +157,15 @@ def tile_moe_pkd_mlp_relu_kernel(
                 start=True,
                 stop=True,
             )
-            nc.scalar.copy(y[:, t0 * P : t1 * P], acc_y[:, 0:width])
+            copy(y[:, t0 * P : t1 * P], acc_y[:, 0:width])
 
         nc.vector.memset(xs[:].bitcast(I32), 0)
+        nc.vector.memset(warm[:, 0:1], 0.0)
         nc.sync.dma_start(offs_t[:], offs)
         load_x_words(0)
         for q in range(4):
             load_x_scales(nc.sync if q < 2 else nc.scalar, q)
+        nc.scalar.activation(warm[:, 1:2], warm[:, 0:1], ACT.Relu)
         load_x_words(1)
         load_x_words(2)
         for e0, e1 in W1_SCALE_CHUNKS[:1]:
@@ -171,57 +178,55 @@ def tile_moe_pkd_mlp_relu_kernel(
         load_w1(0)
         load_w1_scales(nc.scalar, 0)
         make_identity(nc, ident[:])
-        nc.scalar.activation(warm[:], ident[:, 0:8], ACT.Relu)
 
-        gather_words(0, 0, C)
         gather_scales(0, nc.scalar)
-        gather_words(0, C, 2 * C)
+        gather_words(0, 0, C)
         gather_words(1, 0, C)
+        gather_scales(1, nc.scalar)
         gather_words(2, 0, C)
-        load_w1_scales(nc.sync, 1)
         load_w1(1)
+        load_w1_scales(nc.sync, 1)
+        load_w1(2)
+        load_w1_scales(nc.sync, 2)
         nc.sync.dma_start(out=w2w[:].bitcast(I32), in_=w2_words.rearrange("e o p c -> p (e o) c").bitcast(I32))
         w2_rows = w2_scales.rearrange("e o q n -> q (e o) n")
         for q in range(4):
             nc.sync.dma_start(out=w2s[32 * q : 32 * q + 4].bitcast(I32), in_=w2_rows[4 * q : 4 * q + 4].bitcast(I32))
-        load_w1(2)
+        nc.sync.dma_start(pos_t[0][:], pos1)
+        nc.sync.dma_start(pos_t[1][:], pos2)
 
         for e in range(E):
             for tile_index in (2 * e, 2 * e + 1):
                 first_layer(tile_index)
+            final = e == E - 1
             if e >= 1:
-                turn(2 * e - 2, 2 * e, 2 * e)
-            if e >= 3:
-                second_layer(2 * e - 6, 2 * e - 4, 2 * e + 1)
+                turn(2 * e - 2, 2 * e, 2 * e, nc.vector.tensor_copy if final else nc.scalar.copy)
+            if e >= 3 and not final:
+                second_layer(2 * e - 6, 2 * e - 4, 2 * e + 1, nc.scalar.copy)
+            if e == 1:
+                gather_scales(2, nc.sync)
+            if e == 3:
+                gather_scales(3, nc.sync)
             nxt = e + 1
             if nxt < E - 1:
                 for a in range(PASSES):
-                    if (nxt, a) != (1, 0):
-                        gather_words(a, nxt * C, (nxt + 1) * C)
+                    gather_words(a, nxt * C, (nxt + 1) * C)
             elif nxt == E - 1:
                 for half in range(2):
                     for a in range(PASSES):
                         gather_words(a, nxt * C + half * P, nxt * C + (half + 1) * P)
-            if e == 0:
-                gather_scales(1, nc.sync)
-                load_w1_scales(nc.sync, 2)
-                load_w1(3)
-                load_w1(4)
-            if e == 2:
-                gather_scales(2, nc.sync)
-                for later in (5, 6, 7):
-                    load_w1(later)
-                nc.sync.dma_start(pos_t[0][:], pos1)
-                nc.sync.dma_start(pos_t[1][:], pos2)
-                for j in range(2):
-                    nc.sync.dma_start(out=gate_t[j][:], in_=gate[j])
+            if e + 3 < E:
+                load_w1(e + 3)
+            elif e + 3 - E < 2:
+                load_gate(e + 3 - E)
         last = 2 * E
-        second_layer(last - 6, last - 4, last)
-        turn(last - 2, last - 1, last + 1)
-        turn(last - 1, last, last + 2)
-        second_layer(last - 4, last - 2, last + 3)
-        second_layer(last - 2, last - 1, last + 4)
-        second_layer(last - 1, last, last + 5)
+        turn(last - 2, last - 1, last + 1, nc.scalar.copy)
+        turn(last - 1, last, last + 2, nc.scalar.copy)
+        second_layer(last - 8, last - 6, last, nc.vector.tensor_copy)
+        second_layer(last - 6, last - 4, last + 3, nc.vector.tensor_copy)
+        second_layer(last - 4, last - 2, last + 4, nc.scalar.copy)
+        second_layer(last - 2, last - 1, last + 5, nc.scalar.copy)
+        second_layer(last - 1, last, last + 7, nc.scalar.copy)
 
         terms = []
         for t0, t1 in OUT_CHUNKS:

@@ -20,16 +20,25 @@ ALU = mybir.AluOpType
 P = 128
 PASSES = K // 512
 SLOTS = E * C
-SHIFT_ROWS = 112
+HALF = P // 2
 SCALE_CHUNKS = ((0, 1), (1, 3), (3, 5), (5, 8))
-W1_SCALE_CHUNKS = ((0, 1), (1, 4), (4, 8))
+W1_SCALE_CHUNKS = ((0, 2), (2, 5), (5, 8))
+W1_GROUPS = ((0, 1), (1, 2), (2, 4), (4, 6), (6, 8))
 OUT_CHUNKS = ((0, 512), (512, 768), (768, 1024))
+
+
+CFG = {"lay":"A","sc":[[0,2],[2,4],[4,6],[6,8]],"wsc":[[0,2],[2,3],[3,7],[7,8]],"wg":[[0,1],[1,2],[2,3],[3,4],[4,5],[5,6],[6,7],[7,8]],"wbufs":5,"pbufs":3,"gbufs":2,"late":[1,2],"defer":3,"dslot":1,"lag":3,"t6":"v","t7":"a","yc":"vavavavav","oc":[[0,512],[512,768],[768,1024]],"head":[["xw",2,"s"],["offs"],["xw",0,"s"],["xs","ssaa"],["xw",1,"s"],["w1",0,"s"],["zsh","g"],["gw",0,1],["z1",0,"v"],["gw",0,0],["gw",0,2],["z1",3,"g"],["z1",2,"g"],["gs",0,"as"],["w1",1,"s"],["gs",1,"as"],["w1s",0,"a"],["z1",1,"v"],["warm"]],"steps":[[["w1",2,"s"],["w1s",1,"s"],["w1s",2,"a"]],[["w1",4,"s"],["w1s",3,"s"]],[],[],[],[],[],[["gate"]]],"after":[[["id"],["w1",3,"s"],["z2","g"],["gs",2,"ss"]],[],[["w1",5,"s"],["w2s","s"],["w1",6,"a"],["gs",3,"ss"],["w2w","s"]],[],[],[],[["w1",7,"s"]],[["pos"]]],"xm":1}
 
 
 def tile_moe_pkd_mlp_relu_kernel(
     tc, x_words, x_scales, w1_words, w1_scales, w2_words, w2_scales, gate, offs, pos1, pos2, out
 ):
     nc = tc.nc
+    SCALE_CHUNKS = CFG["sc"]
+    W1_SCALE_CHUNKS = CFG["wsc"]
+    W1_GROUPS = CFG["wg"]
+    OUT_CHUNKS = CFG["oc"]
+    Q = {"s": nc.sync, "a": nc.scalar, "g": nc.gpsimd, "v": nc.vector}
     with ExitStack() as ctx:
         keep = ctx.enter_context(tc.tile_pool(name="keep", bufs=1))
         ring = ctx.enter_context(tc.tile_pool(name="ring", bufs=3))
@@ -37,14 +46,18 @@ def tile_moe_pkd_mlp_relu_kernel(
 
         offs_t = keep.tile([P, SLOTS // 16], U16, name="offs_t")
         pos_t = [keep.tile([P, T // 16], U16, name=f"pos_t{j}") for j in range(2)]
-        xw = [keep.tile([P, T], I32, name=f"xw{a}", align_bytes=64) for a in range(PASSES)]
+        if CFG.get("xm"):
+            x0 = keep.tile([P, T], I32, name="xw0", align_bytes=64)
+            x12 = keep.tile([P, 2, T], I32, name="xw1", align_bytes=64)
+            xw = [x0[:], x12[:, 0, :], x12[:, 1, :]]
+        else:
+            xw = [keep.tile([P, T], I32, name=f"xw{a}", align_bytes=64)[:] for a in range(PASSES)]
         xs = keep.tile([P, T], U8, name="xs", align_bytes=64)
         shifted = {a: keep.tile([P, SLOTS], U8, name=f"shifted{a}", align_bytes=64) for a in (1, 2)}
         gw = {}
         gs = {}
         w1w = {}
         w1s = keep.tile([P, E * PASSES, H], U8, name="w1s", align_bytes=64)
-        w2w = keep.tile([P, E, 2 * N], U8, name="w2w", align_bytes=64)
         w2s = keep.tile([P, E, N], U8, name="w2s", align_bytes=64)
         gate_t = {}
         y = keep.tile([P, SLOTS], F32, name="y")
@@ -56,60 +69,87 @@ def tile_moe_pkd_mlp_relu_kernel(
             rows = w1_scales[e0:e1].rearrange("e s q i -> q (e s) i")
             for q in range(4):
                 queue.dma_start(
-                    out=w1s[32 * q : 32 * q + 4, e0 * PASSES : e1 * PASSES, :].bitcast(I32),
-                    in_=rows[4 * q : 4 * q + 4].bitcast(I32),
+                    out=w1s[q:P:32, e0 * PASSES : e1 * PASSES, :].bitcast(I32),
+                    in_=rows[q:16:4].bitcast(I32),
                 )
 
-        def load_gate(j):
-            gate_t[j] = ring.tile([P, T], F32, name=f"gate_t{j}", tag="stream", bufs=3, align_bytes=64)
-            nc.sync.dma_start(out=gate_t[j][:], in_=gate[j])
+        def load_gate():
+            both = ring.tile([P, 2, T], F32, name="gates", tag="stream", bufs=CFG["wbufs"], align_bytes=64)
+            nc.sync.dma_start(out=both[:], in_=gate.rearrange("j p t -> p j t"))
+            for j in range(2):
+                gate_t[j] = both[:, j, :]
 
-        def load_w1(e):
-            w1w[e] = ring.tile([P, PASSES, 2 * H], U8, name=f"w1w{e}", tag="stream", bufs=3, align_bytes=64)
-            nc.sync.dma_start(out=w1w[e][:].bitcast(I32), in_=w1_words[e].rearrange("s p c -> p s c").bitcast(I32))
-
-        def load_x_words(a):
-            nc.sync.dma_start(out=xw[a][:], in_=x_words[a].rearrange("p t r -> p (t r)").bitcast(I32))
-
-        def load_x_scales(queue, q):
+        def load_w1(group, queue):
+            e0, e1 = W1_GROUPS[group]
+            words = ring.tile([P, (e1 - e0) * PASSES, 2 * H], U8, name=f"w1w{e0}", tag="stream", bufs=CFG["wbufs"], align_bytes=64)
             queue.dma_start(
-                out=xs[32 * q : 32 * q + 4 * PASSES, :].bitcast(I32),
-                in_=x_scales[:, 4 * q : 4 * q + 4, :].bitcast(I32),
+                out=words[:].bitcast(I32), in_=w1_words[e0:e1].rearrange("e s p c -> p (e s) c").bitcast(I32)
+            )
+            for e in range(e0, e1):
+                w1w[e] = words[:, (e - e0) * PASSES : (e - e0 + 1) * PASSES, :]
+
+        def load_w1_pass(a, queue):
+            e0, e1 = W1_GROUPS[0]
+            if "h" not in w2:
+                w2["h"] = ring.tile([P, PASSES, e1, 2 * H], U8, name="w1first", tag="stream", bufs=CFG["wbufs"], align_bytes=64)
+                for e in range(e1):
+                    w1w[e] = w2["h"][:, :, e, :]
+            queue.dma_start(out=w2["h"][:, a].bitcast(I32), in_=w1_words[0:e1, a].rearrange("e p c -> p e c").bitcast(I32))
+
+        def load_x_scales(queue, q, a0, a1, row):
+            queue.dma_start(
+                out=xs[row : row + 4 * (a1 - a0), :].bitcast(I32),
+                in_=x_scales[a0:a1, 4 * q : 4 * q + 4, :].bitcast(I32),
             )
 
         def gather_scales(chunk, queue):
             e0, e1 = SCALE_CHUNKS[chunk]
             width = (e1 - e0) * C
-            packed = ring.tile([P, 3 * C], U8, name="packed", bufs=2, align_bytes=64)
+            packed = ring.tile([P, width], U8, name="packed", bufs=CFG["pbufs"], align_bytes=64)
             nc.vector.tensor_copy(packed[:, 0:width], xs[:].indirect(offs_t[:, e0 * C // 16 : e1 * C // 16]))
             for e in range(e0, e1):
                 gs[e] = packed[:, (e - e0) * C : (e - e0 + 1) * C]
             for a in (1, 2):
-                queue.dma_start(
-                    out=shifted[a][0:SHIFT_ROWS, e0 * C : e1 * C].bitcast(I32),
-                    in_=packed[4 * a : 4 * a + SHIFT_ROWS, 0:width].bitcast(I32),
-                )
+                if CFG["lay"] == "A":
+                    Q[queue[a - 1]].dma_start(
+                        out=shifted[a][0:112, e0 * C : e1 * C].bitcast(I32),
+                        in_=packed[4 * a : 4 * a + 112, 0:width].bitcast(I32),
+                    )
+                    continue
+                for row, source in ((0, 4 * a), (HALF, HALF + 4 * a - 4 * PASSES)):
+                    Q[queue[a - 1]].dma_start(
+                        out=shifted[a][row : row + HALF, e0 * C : e1 * C].bitcast(I32),
+                        in_=packed[source : source + HALF, 0:width].bitcast(I32),
+                    )
 
         def gather_words(a, s0, s1):
             e = s0 // C
-            if (e, a) not in gw:
-                gw[e, a] = ring.tile([P, C], U32, name=f"gw{a}", bufs=2, align_bytes=64)
+            if (e, a) == tuple(CFG["late"]):
+                gw[e, a] = keep.tile([P, C], U32, name="gw_first", tag="late", align_bytes=64)
+            elif (e, a) not in gw:
+                gw[e, a] = ring.tile([P, C], U32, name=f"gw{a}", bufs=CFG["gbufs"], align_bytes=64)
             nc.vector.tensor_copy(
-                gw[e, a][:, s0 - e * C : s1 - e * C], xw[a][:].bitcast(U32).indirect(offs_t[:, s0 // 16 : s1 // 16])
+                gw[e, a][:, s0 - e * C : s1 - e * C], xw[a].bitcast(U32).indirect(offs_t[:, s0 // 16 : s1 // 16])
             )
 
         def bank(index):
             return psum.tile([P, H], F32, name=f"bank{index % 8}")
 
+        late_codes = {}
+        w2 = {}
         hidden = {}
         grouped = {}
 
-        def first_layer(tile_index):
+        accs = {}
+
+        def first_layer(tile_index, passes=range(PASSES)):
             e = tile_index * P // C
             cols = slice(tile_index * P, (tile_index + 1) * P)
             own = slice(tile_index * P - e * C, (tile_index + 1) * P - e * C)
-            acc = bank(tile_index)
-            for a in range(PASSES):
+            if tile_index not in accs:
+                accs[tile_index] = bank(tile_index)
+            acc = accs[tile_index]
+            for a in passes:
                 nc.tensor.matmul_mx(
                     out=acc[:],
                     lhsT=gw[e, a][:, own].bitcast(FP8X4),
@@ -119,7 +159,9 @@ def tile_moe_pkd_mlp_relu_kernel(
                     start=(a == 0),
                     stop=(a == PASSES - 1),
                 )
-            h = ring.tile([P, H], BF16, name="h", bufs=6, align_bytes=64)
+            if PASSES - 1 not in passes:
+                return
+            h = ring.tile([P, H], BF16, name="h", bufs=8, align_bytes=64)
             nc.scalar.activation(
                 h[:].rearrange("s (u p d) -> s u p d", u=2, d=2),
                 acc[:].rearrange("s (p u d) -> s u p d", u=2, d=2),
@@ -134,15 +176,21 @@ def tile_moe_pkd_mlp_relu_kernel(
                 words = hidden[t0 + j][:].bitcast(F32)
                 for u in range(2):
                     nc.tensor.transpose(turned[:, j, u, :], words[:, u * P : (u + 1) * P], ident[:])
-            g = ring.tile([P, 2, P, 2], F32, name="g", bufs=5, align_bytes=64)
+            g = ring.tile([P, 2, P, 2], F32, name="g", bufs=8, align_bytes=64)
             copy(g[:, 0:tiles], turned[:, 0:tiles].rearrange("p j u s -> p j s u"))
             grouped[t0] = g
 
         def second_layer(t0, t1, bank_index, copy):
             width = (t1 - t0) * P
             e = t0 * P // C
-            codes = ring.tile([P, C], U32, name="codes", align_bytes=64)
-            scales = ring.tile([P, C], U8, name="scales", align_bytes=64)
+            if e >= CFG["defer"] and e < E - 2:
+                slot = CFG["dslot"]
+                if "t" not in late_codes:
+                    late_codes["t"] = keep.tile([P, T], U32, name="late_codes", tag=f"xw{slot}", align_bytes=64)
+                codes = late_codes["t"][:, (e % 4) * C : (e % 4 + 1) * C]
+            else:
+                codes = ring.tile([P, C], U32, name="codes", align_bytes=64)
+            scales = ring.tile([P, C], U8, name="scales", bufs=6, align_bytes=64)
             values = grouped[t0][:].rearrange("p j s u -> p (j s u)").bitcast(BF16)
             nc.vector.quantize_mx(
                 out=codes[:, 0:width].bitcast(FP8X4), scales=scales[:, 0:width], in_=values[:, 0 : 4 * width]
@@ -150,7 +198,7 @@ def tile_moe_pkd_mlp_relu_kernel(
             acc_y = bank(bank_index)
             nc.tensor.matmul_mx(
                 out=acc_y[:, 0:width],
-                lhsT=w2w[:, e, :].bitcast(FP4X4),
+                lhsT=w2["w"][:, e, :].bitcast(FP4X4),
                 lhsT_scale=w2s[:, e, :],
                 rhs=codes[:, 0:width].bitcast(FP8X4),
                 rhs_scale=scales[:, 0:width],
@@ -159,74 +207,108 @@ def tile_moe_pkd_mlp_relu_kernel(
             )
             copy(y[:, t0 * P : t1 * P], acc_y[:, 0:width])
 
-        nc.vector.memset(xs[:].bitcast(I32), 0)
-        nc.vector.memset(warm[:, 0:1], 0.0)
-        nc.sync.dma_start(offs_t[:], offs)
-        load_x_words(0)
-        for q in range(4):
-            load_x_scales(nc.sync if q < 2 else nc.scalar, q)
-        nc.scalar.activation(warm[:, 1:2], warm[:, 0:1], ACT.Relu)
-        load_x_words(1)
-        load_x_words(2)
-        for e0, e1 in W1_SCALE_CHUNKS[:1]:
-            nc.vector.memset(w1s[:, e0 * PASSES : e1 * PASSES, :].bitcast(I32), 0)
-        for a in (1, 2):
-            nc.vector.memset(shifted[a][:].bitcast(I32), 0)
-        for e0, e1 in W1_SCALE_CHUNKS[1:]:
-            nc.vector.memset(w1s[:, e0 * PASSES : e1 * PASSES, :].bitcast(I32), 0)
-        nc.vector.memset(w2s[:].bitcast(I32), 0)
-        load_w1(0)
-        load_w1_scales(nc.scalar, 0)
-        make_identity(nc, ident[:])
+        def zero_w1_scales(engine, chunk):
+            e0, e1 = W1_SCALE_CHUNKS[chunk]
+            engine.memset(w1s[:, e0 * PASSES : e1 * PASSES, :].bitcast(I32), 0)
 
-        gather_scales(0, nc.scalar)
-        gather_words(0, 0, C)
-        gather_words(1, 0, C)
-        gather_scales(1, nc.scalar)
-        gather_words(2, 0, C)
-        load_w1(1)
-        load_w1_scales(nc.sync, 1)
-        load_w1(2)
-        load_w1_scales(nc.sync, 2)
-        nc.sync.dma_start(out=w2w[:].bitcast(I32), in_=w2_words.rearrange("e o p c -> p (e o) c").bitcast(I32))
+        x_rows = x_words.rearrange("a p t r -> p a (t r)").bitcast(I32)
         w2_rows = w2_scales.rearrange("e o q n -> q (e o) n")
-        for q in range(4):
-            nc.sync.dma_start(out=w2s[32 * q : 32 * q + 4].bitcast(I32), in_=w2_rows[4 * q : 4 * q + 4].bitcast(I32))
-        nc.sync.dma_start(pos_t[0][:], pos1)
-        nc.sync.dma_start(pos_t[1][:], pos2)
+        XS = {"A": [(0, 0, 3, 0), (1, 0, 3, 32), (2, 0, 3, 64), (3, 0, 3, 96)],
+              "B": [(0, 0, 3, 0), (1, 0, 3, 32), (2, 0, 1, 64), (2, 1, 3, 56), (3, 0, 1, 96), (3, 1, 3, 88)],
+              "C": [(0, 0, 1, 0), (0, 1, 3, 4), (1, 0, 1, 32), (1, 1, 3, 36), (2, 0, 1, 64), (2, 1, 3, 56), (3, 0, 1, 96), (3, 1, 3, 88)]}[CFG["lay"]]
 
+        def do(tok):
+            k = tok[0]
+            if k == "offs":
+                nc.sync.dma_start(offs_t[:], offs)
+            elif k == "pos":
+                nc.sync.dma_start(pos_t[0][:], pos1)
+                nc.sync.dma_start(pos_t[1][:], pos2)
+            elif k == "xw":
+                if CFG.get("xm") and tok[1] == 1:
+                    Q[tok[2]].dma_start(out=x12[:], in_=x_rows[:, 1:3, :])
+                elif not (CFG.get("xm") and tok[1] == 2):
+                    Q[tok[2]].dma_start(out=xw[tok[1]], in_=x_rows[:, tok[1], :])
+            elif k == "xs":
+                for n, spec in enumerate(XS):
+                    load_x_scales(Q[tok[1][n]], *spec)
+            elif k == "w1":
+                if tok[1] < len(W1_GROUPS):
+                    load_w1(tok[1], Q[tok[2]])
+            elif k == "w1p":
+                load_w1_pass(tok[1], Q[tok[2]])
+            elif k == "w1s":
+                if tok[1] < len(W1_SCALE_CHUNKS):
+                    load_w1_scales(Q[tok[2]], tok[1])
+            elif k == "z1":
+                if tok[1] < len(W1_SCALE_CHUNKS):
+                    zero_w1_scales(Q[tok[2]], tok[1])
+            elif k == "zsh":
+                if CFG["lay"] == "A":
+                    for a in (1, 2):
+                        Q[tok[1]].memset(shifted[a][:].bitcast(I32), 0)
+            elif k == "z2":
+                Q[tok[1]].memset(w2s[:].bitcast(I32), 0)
+            elif k == "id":
+                make_identity(nc, ident[:])
+            elif k == "warm":
+                nc.vector.memset(warm[:, 0:1], 0.0)
+                nc.scalar.activation(warm[:, 1:2], warm[:, 0:1], ACT.Relu)
+            elif k == "gs":
+                if tok[1] < len(SCALE_CHUNKS):
+                    gather_scales(tok[1], tok[2])
+            elif k == "gw":
+                gather_words(tok[2], tok[1] * C, (tok[1] + 1) * C)
+            elif k == "w2w":
+                w2["w"] = keep.tile([P, E, 2 * N], U8, name="w2w", tag="late", align_bytes=64)
+                Q[tok[1]].dma_start(out=w2["w"][:].bitcast(I32), in_=w2_words.rearrange("e o p c -> p (e o) c").bitcast(I32))
+            elif k == "w2s":
+                for q in range(4):
+                    Q[tok[1]].dma_start(out=w2s[q:P:32].bitcast(I32), in_=w2_rows[q:16:4].bitcast(I32))
+            elif k == "gate":
+                load_gate()
+
+        nc.vector.memset(xs[:].bitcast(I32), 0)
+        for tok in CFG["head"]:
+            do(tok)
+        lag = CFG["lag"]
+        eng = {"a": nc.scalar.copy, "v": nc.vector.tensor_copy}
+        ndone = 0
         for e in range(E):
-            for tile_index in (2 * e, 2 * e + 1):
-                first_layer(tile_index)
+            G = W1_GROUPS[0][1] if CFG.get("pm") else 0
+            if e == 0 and G:
+                for a in range(PASSES):
+                    for tile_index in range(2 * G):
+                        first_layer(tile_index, [a])
+            if e >= G:
+                for tile_index in (2 * e, 2 * e + 1):
+                    first_layer(tile_index)
             final = e == E - 1
             if e >= 1:
-                turn(2 * e - 2, 2 * e, 2 * e, nc.vector.tensor_copy if final else nc.scalar.copy)
-            if e >= 3 and not final:
-                second_layer(2 * e - 6, 2 * e - 4, 2 * e + 1, nc.scalar.copy)
-            if e == 1:
-                gather_scales(2, nc.sync)
-            if e == 3:
-                gather_scales(3, nc.sync)
+                turn(2 * e - 2, 2 * e, 2 * e, eng[CFG["t6"]] if final else nc.scalar.copy)
+            if e >= lag and not final and e - lag < CFG["defer"]:
+                second_layer(2 * (e - lag), 2 * (e - lag) + 2, 2 * e + 1, nc.scalar.copy)
+                ndone = e - lag + 1
+            for tok in CFG["steps"][e]:
+                do(tok)
             nxt = e + 1
             if nxt < E - 1:
                 for a in range(PASSES):
-                    gather_words(a, nxt * C, (nxt + 1) * C)
+                    if (nxt, a) not in gw:
+                        gather_words(a, nxt * C, (nxt + 1) * C)
             elif nxt == E - 1:
                 for half in range(2):
                     for a in range(PASSES):
                         gather_words(a, nxt * C + half * P, nxt * C + (half + 1) * P)
-            if e + 3 < E:
-                load_w1(e + 3)
-            elif e + 3 - E < 2:
-                load_gate(e + 3 - E)
+            for tok in CFG["after"][e]:
+                do(tok)
         last = 2 * E
         turn(last - 2, last - 1, last + 1, nc.scalar.copy)
-        turn(last - 1, last, last + 2, nc.scalar.copy)
-        second_layer(last - 8, last - 6, last, nc.vector.tensor_copy)
-        second_layer(last - 6, last - 4, last + 3, nc.vector.tensor_copy)
-        second_layer(last - 4, last - 2, last + 4, nc.scalar.copy)
-        second_layer(last - 2, last - 1, last + 5, nc.scalar.copy)
-        second_layer(last - 1, last, last + 7, nc.scalar.copy)
+        turn(last - 1, last, last + 2, eng[CFG["t7"]])
+        free_banks = [0, 3, 4, 5, 7, 6, 1, 2, 0, 3]
+        rest = [(2 * e, 2 * e + 2) for e in range(ndone, E - 1)] + [(last - 2, last - 1), (last - 1, last)]
+        for n, unit in enumerate(rest):
+            second_layer(unit[0], unit[1], free_banks[n], eng[CFG["yc"][len(CFG["yc"]) - len(rest) + n]])
 
         terms = []
         for t0, t1 in OUT_CHUNKS:

@@ -27,7 +27,7 @@ W1_GROUPS = ((0, 1), (1, 2), (2, 4), (4, 6), (6, 8))
 OUT_CHUNKS = ((0, 512), (512, 768), (768, 1024))
 
 
-CFG = {"lay":"A","sc":[[0,2],[2,4],[4,6],[6,8]],"wsc":[[0,2],[2,3],[3,7],[7,8]],"wg":[[0,1],[1,2],[2,3],[3,4],[4,5],[5,6],[6,7],[7,8]],"wbufs":5,"pbufs":3,"gbufs":2,"late":[1,2],"defer":3,"dslot":1,"lag":3,"t6":"v","t7":"a","yc":"vavavavav","oc":[[0,512],[512,768],[768,1024]],"head":[["xw",2,"s"],["offs"],["xw",0,"s"],["xs","ssaa"],["xw",1,"s"],["w1",0,"s"],["zsh","g"],["gw",0,1],["z1",0,"v"],["gw",0,0],["gw",0,2],["z1",3,"g"],["z1",2,"g"],["gs",0,"as"],["w1",1,"s"],["gs",1,"as"],["w1s",0,"a"],["z1",1,"v"],["warm"]],"steps":[[["w1",2,"s"],["w1s",1,"s"],["w1s",2,"a"]],[["w1",4,"s"],["w1s",3,"s"]],[],[],[],[],[],[["gate"]]],"after":[[["id"],["w1",3,"s"],["z2","g"],["gs",2,"ss"]],[],[["w1",5,"s"],["w2s","s"],["w1",6,"a"],["gs",3,"ss"],["w2w","s"]],[],[],[],[["w1",7,"s"]],[["pos"]]],"xm":1}
+CFG = {"lay":"A","sc":[[0,1],[1,4],[4,5],[5,8]],"wsc":[[0,3],[3,7],[7,8]],"wg":[[0,1],[1,2],[2,3],[3,4],[4,5],[5,6],[6,7],[7,8]],"wbufs":5,"pbufs":3,"gbufs":3,"late":[0,1],"defer":2,"dslot":0,"lag":4,"t6":"v","t7":"a","yc":"avaavaaaa","oc":[[0,640],[640,896],[896,1024]],"head":[["z1",0,"g"],["offs"],["xw",0,"s"],["xs","sasa"],["xw",1,"s"],["w1",0,"s"],["w1",1,"s"],["zsh","v"],["z2","g"],["gs",0,"sa"],["gw",0,2],["w1s",0,"g"],["w1",2,"s"],["warm"],["gs",1,"sa"],["xw",2,"a"],["z1",1,"v"],["w1",3,"s"],["gw",0,0],["gw",0,1]],"steps":[[["w1s",1,"s"]],[["gs",3,"ss"]],[["w1",5,"s"]],[["w1",6,"s"],["pos"]],[],[],[["gate"]],[]],"after":[[["w1",4,"s"],["id"],["gs",2,"ss"]],[["z1",2,"v"]],[],[["w2s","s"],["w1",7,"s"],["w1s",2,"s"],["w2w","s"]],[],[],[],[]],"xm":1,"tc":"aaaaaa","ys":"aaaa","rc":"aaaa"}
 
 
 def tile_moe_pkd_mlp_relu_kernel(
@@ -67,10 +67,10 @@ def tile_moe_pkd_mlp_relu_kernel(
         def load_w1_scales(queue, chunk):
             e0, e1 = W1_SCALE_CHUNKS[chunk]
             rows = w1_scales[e0:e1].rearrange("e s q i -> q (e s) i")
-            for q in range(4):
+            for q in (0, 2, 1, 3):
                 queue.dma_start(
-                    out=w1s[q:P:32, e0 * PASSES : e1 * PASSES, :].bitcast(I32),
-                    in_=rows[q:16:4].bitcast(I32),
+                    out=w1s[32 * q : 32 * q + 4, e0 * PASSES : e1 * PASSES, :].bitcast(I32),
+                    in_=rows[4 * q : 4 * q + 4].bitcast(I32),
                 )
 
         def load_gate():
@@ -162,11 +162,12 @@ def tile_moe_pkd_mlp_relu_kernel(
             if PASSES - 1 not in passes:
                 return
             h = ring.tile([P, H], BF16, name="h", bufs=8, align_bytes=64)
-            nc.scalar.activation(
-                h[:].rearrange("s (u p d) -> s u p d", u=2, d=2),
-                acc[:].rearrange("s (p u d) -> s u p d", u=2, d=2),
-                ACT.Relu,
-            )
+            h_out = h[:].rearrange("s (u p d) -> s u p d", u=2, d=2)
+            h_in = acc[:].rearrange("s (p u d) -> s u p d", u=2, d=2)
+            if tile_index >= 12 and CFG.get("rc", "aaaa")[tile_index - 12] == "v":
+                nc.vector.tensor_scalar_max(h_out, h_in, 0.0)
+            else:
+                nc.scalar.activation(h_out, h_in, ACT.Relu)
             hidden[tile_index] = h
 
         def turn(t0, t1, bank_index, copy):
@@ -264,7 +265,7 @@ def tile_moe_pkd_mlp_relu_kernel(
                 Q[tok[1]].dma_start(out=w2["w"][:].bitcast(I32), in_=w2_words.rearrange("e o p c -> p (e o) c").bitcast(I32))
             elif k == "w2s":
                 for q in range(4):
-                    Q[tok[1]].dma_start(out=w2s[q:P:32].bitcast(I32), in_=w2_rows[q:16:4].bitcast(I32))
+                    Q[tok[1]].dma_start(out=w2s[32 * q : 32 * q + 4].bitcast(I32), in_=w2_rows[4 * q : 4 * q + 4].bitcast(I32))
             elif k == "gate":
                 load_gate()
 
@@ -285,9 +286,9 @@ def tile_moe_pkd_mlp_relu_kernel(
                     first_layer(tile_index)
             final = e == E - 1
             if e >= 1:
-                turn(2 * e - 2, 2 * e, 2 * e, eng[CFG["t6"]] if final else nc.scalar.copy)
+                turn(2 * e - 2, 2 * e, 2 * e, eng[CFG["t6"]] if final else eng[CFG.get("tc", "aaaaaa")[e - 1]])
             if e >= lag and not final and e - lag < CFG["defer"]:
-                second_layer(2 * (e - lag), 2 * (e - lag) + 2, 2 * e + 1, nc.scalar.copy)
+                second_layer(2 * (e - lag), 2 * (e - lag) + 2, 2 * e + 1, eng[CFG.get("ys", "aaaa")[e - lag]])
                 ndone = e - lag + 1
             for tok in CFG["steps"][e]:
                 do(tok)

from contextlib import ExitStack

import concourse.mybir as mybir
from concourse.masks import make_identity

K, T, E, C, H, N = 1536, 1024, 8, 256, 512, 128
FLOPS = 2 * E * C * (K * H + H * N)

F32 = mybir.dt.float32
BF16 = mybir.dt.bfloat16
I32 = mybir.dt.int32
U32 = mybir.dt.uint32
U16 = mybir.dt.uint16
U8 = mybir.dt.uint8
FP8X4 = mybir.dt.float8_e4m3fn_x4
FP4X4 = mybir.dt.float4_e2m1fn_x4
ACT = mybir.ActivationFunctionType
ALU = mybir.AluOpType

P = 128
PASSES = K // 512
SLOTS = E * C
HALF = P // 2
SCALE_CHUNKS = ((0, 1), (1, 3), (3, 5), (5, 8))
W1_SCALE_CHUNKS = ((0, 2), (2, 5), (5, 8))
W1_GROUPS = ((0, 1), (1, 2), (2, 4), (4, 6), (6, 8))
OUT_CHUNKS = ((0, 512), (512, 768), (768, 1024))


CFG = {"lay":"A","sc":[[0,1],[1,4],[4,5],[5,8]],"wsc":[[0,3],[3,7],[7,8]],"wg":[[0,1],[1,2],[2,3],[3,4],[4,5],[5,6],[6,7],[7,8]],"wbufs":5,"pbufs":3,"gbufs":3,"late":[0,1],"defer":2,"dslot":0,"lag":4,"t6":"v","t7":"a","yc":"avaavaaaa","oc":[[0,640],[640,896],[896,1024]],"head":[["z1",0,"g"],["offs"],["xw",0,"s"],["xs","sasa"],["xw",1,"s"],["w1",0,"s"],["w1",1,"s"],["zsh","v"],["z2","g"],["gs",0,"sa"],["gw",0,2],["w1s",0,"g"],["w1",2,"s"],["warm"],["gs",1,"sa"],["xw",2,"a"],["z1",1,"v"],["w1",3,"s"],["gw",0,0],["gw",0,1]],"steps":[[["w1s",1,"s"]],[["gs",3,"ss"]],[["w1",5,"s"]],[["w1",6,"s"],["pos"]],[],[],[["gate"]],[]],"after":[[["w1",4,"s"],["id"],["gs",2,"ss"]],[["z1",2,"v"]],[],[["w2s","s"],["w1",7,"s"],["w1s",2,"s"],["w2w","s"]],[],[],[],[]],"xm":1,"tc":"aaaaaa","ys":"aaaa","rc":"aaaa"}


def tile_moe_pkd_mlp_relu_kernel(
    tc, x_words, x_scales, w1_words, w1_scales, w2_words, w2_scales, gate, offs, pos1, pos2, out
):
    nc = tc.nc
    SCALE_CHUNKS = CFG["sc"]
    W1_SCALE_CHUNKS = CFG["wsc"]
    W1_GROUPS = CFG["wg"]
    OUT_CHUNKS = CFG["oc"]
    Q = {"s": nc.sync, "a": nc.scalar, "g": nc.gpsimd, "v": nc.vector}
    with ExitStack() as ctx:
        keep = ctx.enter_context(tc.tile_pool(name="keep", bufs=1))
        ring = ctx.enter_context(tc.tile_pool(name="ring", bufs=3))
        psum = ctx.enter_context(tc.psum_pool(name="psum", bufs=1))

        offs_t = keep.tile([P, SLOTS // 16], U16, name="offs_t")
        pos_t = [keep.tile([P, T // 16], U16, name=f"pos_t{j}") for j in range(2)]
        if CFG.get("xm"):
            x0 = keep.tile([P, T], I32, name="xw0", align_bytes=64)
            x12 = keep.tile([P, 2, T], I32, name="xw1", align_bytes=64)
            xw = [x0[:], x12[:, 0, :], x12[:, 1, :]]
        else:
            xw = [keep.tile([P, T], I32, name=f"xw{a}", align_bytes=64)[:] for a in range(PASSES)]
        xs = keep.tile([P, T], U8, name="xs", align_bytes=64)
        shifted = {a: keep.tile([P, SLOTS], U8, name=f"shifted{a}", align_bytes=64) for a in (1, 2)}
        gw = {}
        gs = {}
        w1w = {}
        w1s = keep.tile([P, E * PASSES, H], U8, name="w1s", align_bytes=64)
        w2s = keep.tile([P, E, N], U8, name="w2s", align_bytes=64)
        gate_t = {}
        y = keep.tile([P, SLOTS], F32, name="y")
        ident = keep.tile([P, P], F32, name="ident")
        warm = keep.tile([P, 8], F32, name="warm")

        def load_w1_scales(queue, chunk):
            e0, e1 = W1_SCALE_CHUNKS[chunk]
            rows = w1_scales[e0:e1].rearrange("e s q i -> q (e s) i")
            for q in (0, 2, 1, 3):
                queue.dma_start(
                    out=w1s[32 * q : 32 * q + 4, e0 * PASSES : e1 * PASSES, :].bitcast(I32),
                    in_=rows[4 * q : 4 * q + 4].bitcast(I32),
                )

        def load_gate():
            both = ring.tile([P, 2, T], F32, name="gates", tag="stream", bufs=CFG["wbufs"], align_bytes=64)
            nc.sync.dma_start(out=both[:], in_=gate.rearrange("j p t -> p j t"))
            for j in range(2):
                gate_t[j] = both[:, j, :]

        def load_w1(group, queue):
            e0, e1 = W1_GROUPS[group]
            words = ring.tile([P, (e1 - e0) * PASSES, 2 * H], U8, name=f"w1w{e0}", tag="stream", bufs=CFG["wbufs"], align_bytes=64)
            queue.dma_start(
                out=words[:].bitcast(I32), in_=w1_words[e0:e1].rearrange("e s p c -> p (e s) c").bitcast(I32)
            )
            for e in range(e0, e1):
                w1w[e] = words[:, (e - e0) * PASSES : (e - e0 + 1) * PASSES, :]

        def load_w1_pass(a, queue):
            e0, e1 = W1_GROUPS[0]
            if "h" not in w2:
                w2["h"] = ring.tile([P, PASSES, e1, 2 * H], U8, name="w1first", tag="stream", bufs=CFG["wbufs"], align_bytes=64)
                for e in range(e1):
                    w1w[e] = w2["h"][:, :, e, :]
            queue.dma_start(out=w2["h"][:, a].bitcast(I32), in_=w1_words[0:e1, a].rearrange("e p c -> p e c").bitcast(I32))

        def load_x_scales(queue, q, a0, a1, row):
            queue.dma_start(
                out=xs[row : row + 4 * (a1 - a0), :].bitcast(I32),
                in_=x_scales[a0:a1, 4 * q : 4 * q + 4, :].bitcast(I32),
            )

        def gather_scales(chunk, queue):
            e0, e1 = SCALE_CHUNKS[chunk]
            width = (e1 - e0) * C
            packed = ring.tile([P, width], U8, name="packed", bufs=CFG["pbufs"], align_bytes=64)
            nc.vector.tensor_copy(packed[:, 0:width], xs[:].indirect(offs_t[:, e0 * C // 16 : e1 * C // 16]))
            for e in range(e0, e1):
                gs[e] = packed[:, (e - e0) * C : (e - e0 + 1) * C]
            for a in (1, 2):
                if CFG["lay"] == "A":
                    Q[queue[a - 1]].dma_start(
                        out=shifted[a][0:112, e0 * C : e1 * C].bitcast(I32),
                        in_=packed[4 * a : 4 * a + 112, 0:width].bitcast(I32),
                    )
                    continue
                for row, source in ((0, 4 * a), (HALF, HALF + 4 * a - 4 * PASSES)):
                    Q[queue[a - 1]].dma_start(
                        out=shifted[a][row : row + HALF, e0 * C : e1 * C].bitcast(I32),
                        in_=packed[source : source + HALF, 0:width].bitcast(I32),
                    )

        def gather_words(a, s0, s1):
            e = s0 // C
            if (e, a) == tuple(CFG["late"]):
                gw[e, a] = keep.tile([P, C], U32, name="gw_first", tag="late", align_bytes=64)
            elif (e, a) not in gw:
                gw[e, a] = ring.tile([P, C], U32, name=f"gw{a}", bufs=CFG["gbufs"], align_bytes=64)
            nc.vector.tensor_copy(
                gw[e, a][:, s0 - e * C : s1 - e * C], xw[a].bitcast(U32).indirect(offs_t[:, s0 // 16 : s1 // 16])
            )

        def bank(index):
            return psum.tile([P, H], F32, name=f"bank{index % 8}")

        late_codes = {}
        w2 = {}
        hidden = {}
        grouped = {}

        accs = {}

        def first_layer(tile_index, passes=range(PASSES)):
            e = tile_index * P // C
            cols = slice(tile_index * P, (tile_index + 1) * P)
            own = slice(tile_index * P - e * C, (tile_index + 1) * P - e * C)
            if tile_index not in accs:
                accs[tile_index] = bank(tile_index)
            acc = accs[tile_index]
            for a in passes:
                nc.tensor.matmul_mx(
                    out=acc[:],
                    lhsT=gw[e, a][:, own].bitcast(FP8X4),
                    lhsT_scale=gs[e][:, own] if a == 0 else shifted[a][:, cols],
                    rhs=w1w[e][:, a, :].bitcast(FP4X4),
                    rhs_scale=w1s[:, e * PASSES + a, :],
                    start=(a == 0),
                    stop=(a == PASSES - 1),
                )
            if PASSES - 1 not in passes:
                return
            h = ring.tile([P, H], BF16, name="h", bufs=8, align_bytes=64)
            h_out = h[:].rearrange("s (u p d) -> s u p d", u=2, d=2)
            h_in = acc[:].rearrange("s (p u d) -> s u p d", u=2, d=2)
            if tile_index >= 12 and CFG.get("rc", "aaaa")[tile_index - 12] == "v":
                nc.vector.tensor_scalar_max(h_out, h_in, 0.0)
            else:
                nc.scalar.activation(h_out, h_in, ACT.Relu)
            hidden[tile_index] = h

        def turn(t0, t1, bank_index, copy):
            tiles = t1 - t0
            turned = bank(bank_index)[:].rearrange("p (j u s) -> p j u s", j=2, u=2)
            for j in range(tiles):
                words = hidden[t0 + j][:].bitcast(F32)
                for u in range(2):
                    nc.tensor.transpose(turned[:, j, u, :], words[:, u * P : (u + 1) * P], ident[:])
            g = ring.tile([P, 2, P, 2], F32, name="g", bufs=8, align_bytes=64)
            copy(g[:, 0:tiles], turned[:, 0:tiles].rearrange("p j u s -> p j s u"))
            grouped[t0] = g

        def second_layer(t0, t1, bank_index, copy):
            width = (t1 - t0) * P
            e = t0 * P // C
            if e >= CFG["defer"] and e < E - 2:
                slot = CFG["dslot"]
                if "t" not in late_codes:
                    late_codes["t"] = keep.tile([P, T], U32, name="late_codes", tag=f"xw{slot}", align_bytes=64)
                codes = late_codes["t"][:, (e % 4) * C : (e % 4 + 1) * C]
            else:
                codes = ring.tile([P, C], U32, name="codes", align_bytes=64)
            scales = ring.tile([P, C], U8, name="scales", bufs=6, align_bytes=64)
            values = grouped[t0][:].rearrange("p j s u -> p (j s u)").bitcast(BF16)
            nc.vector.quantize_mx(
                out=codes[:, 0:width].bitcast(FP8X4), scales=scales[:, 0:width], in_=values[:, 0 : 4 * width]
            )
            acc_y = bank(bank_index)
            nc.tensor.matmul_mx(
                out=acc_y[:, 0:width],
                lhsT=w2["w"][:, e, :].bitcast(FP4X4),
                lhsT_scale=w2s[:, e, :],
                rhs=codes[:, 0:width].bitcast(FP8X4),
                rhs_scale=scales[:, 0:width],
                start=True,
                stop=True,
            )
            copy(y[:, t0 * P : t1 * P], acc_y[:, 0:width])

        def zero_w1_scales(engine, chunk):
            e0, e1 = W1_SCALE_CHUNKS[chunk]
            engine.memset(w1s[:, e0 * PASSES : e1 * PASSES, :].bitcast(I32), 0)

        x_rows = x_words.rearrange("a p t r -> p a (t r)").bitcast(I32)
        w2_rows = w2_scales.rearrange("e o q n -> q (e o) n")
        XS = {"A": [(0, 0, 3, 0), (1, 0, 3, 32), (2, 0, 3, 64), (3, 0, 3, 96)],
              "B": [(0, 0, 3, 0), (1, 0, 3, 32), (2, 0, 1, 64), (2, 1, 3, 56), (3, 0, 1, 96), (3, 1, 3, 88)],
              "C": [(0, 0, 1, 0), (0, 1, 3, 4), (1, 0, 1, 32), (1, 1, 3, 36), (2, 0, 1, 64), (2, 1, 3, 56), (3, 0, 1, 96), (3, 1, 3, 88)]}[CFG["lay"]]

        def do(tok):
            k = tok[0]
            if k == "offs":
                nc.sync.dma_start(offs_t[:], offs)
            elif k == "pos":
                nc.sync.dma_start(pos_t[0][:], pos1)
                nc.sync.dma_start(pos_t[1][:], pos2)
            elif k == "xw":
                if CFG.get("xm") and tok[1] == 1:
                    Q[tok[2]].dma_start(out=x12[:], in_=x_rows[:, 1:3, :])
                elif not (CFG.get("xm") and tok[1] == 2):
                    Q[tok[2]].dma_start(out=xw[tok[1]], in_=x_rows[:, tok[1], :])
            elif k == "xs":
                for n, spec in enumerate(XS):
                    load_x_scales(Q[tok[1][n]], *spec)
            elif k == "w1":
                if tok[1] < len(W1_GROUPS):
                    load_w1(tok[1], Q[tok[2]])
            elif k == "w1p":
                load_w1_pass(tok[1], Q[tok[2]])
            elif k == "w1s":
                if tok[1] < len(W1_SCALE_CHUNKS):
                    load_w1_scales(Q[tok[2]], tok[1])
            elif k == "z1":
                if tok[1] < len(W1_SCALE_CHUNKS):
                    zero_w1_scales(Q[tok[2]], tok[1])
            elif k == "zsh":
                if CFG["lay"] == "A":
                    for a in (1, 2):
                        Q[tok[1]].memset(shifted[a][:].bitcast(I32), 0)
            elif k == "z2":
                Q[tok[1]].memset(w2s[:].bitcast(I32), 0)
            elif k == "id":
                make_identity(nc, ident[:])
            elif k == "warm":
                nc.vector.memset(warm[:, 0:1], 0.0)
                nc.scalar.activation(warm[:, 1:2], warm[:, 0:1], ACT.Relu)
            elif k == "gs":
                if tok[1] < len(SCALE_CHUNKS):
                    gather_scales(tok[1], tok[2])
            elif k == "gw":
                gather_words(tok[2], tok[1] * C, (tok[1] + 1) * C)
            elif k == "w2w":
                w2["w"] = keep.tile([P, E, 2 * N], U8, name="w2w", tag="late", align_bytes=64)
                Q[tok[1]].dma_start(out=w2["w"][:].bitcast(I32), in_=w2_words.rearrange("e o p c -> p (e o) c").bitcast(I32))
            elif k == "w2s":
                for q in range(4):
                    Q[tok[1]].dma_start(out=w2s[32 * q : 32 * q + 4].bitcast(I32), in_=w2_rows[4 * q : 4 * q + 4].bitcast(I32))
            elif k == "gate":
                load_gate()

        nc.vector.memset(xs[:].bitcast(I32), 0)
        for tok in CFG["head"]:
            do(tok)
        lag = CFG["lag"]
        eng = {"a": nc.scalar.copy, "v": nc.vector.tensor_copy}
        ndone = 0
        for e in range(E):
            G = W1_GROUPS[0][1] if CFG.get("pm") else 0
            if e == 0 and G:
                for a in range(PASSES):
                    for tile_index in range(2 * G):
                        first_layer(tile_index, [a])
            if e >= G:
                for tile_index in (2 * e, 2 * e + 1):
                    first_layer(tile_index)
            final = e == E - 1
            if e >= 1:
                turn(2 * e - 2, 2 * e, 2 * e, eng[CFG["t6"]] if final else eng[CFG.get("tc", "aaaaaa")[e - 1]])
            if e >= lag and not final and e - lag < CFG["defer"]:
                second_layer(2 * (e - lag), 2 * (e - lag) + 2, 2 * e + 1, eng[CFG.get("ys", "aaaa")[e - lag]])
                ndone = e - lag + 1
            for tok in CFG["steps"][e]:
                do(tok)
            nxt = e + 1
            if nxt < E - 1:
                for a in range(PASSES):
                    if (nxt, a) not in gw:
                        gather_words(a, nxt * C, (nxt + 1) * C)
            elif nxt == E - 1:
                for half in range(2):
                    for a in range(PASSES):
                        gather_words(a, nxt * C + half * P, nxt * C + (half + 1) * P)
            for tok in CFG["after"][e]:
                do(tok)
        last = 2 * E
        turn(last - 2, last - 1, last + 1, nc.scalar.copy)
        turn(last - 1, last, last + 2, eng[CFG["t7"]])
        free_banks = [0, 3, 4, 5, 7, 6, 1, 2, 0, 3]
        rest = [(2 * e, 2 * e + 2) for e in range(ndone, E - 1)] + [(last - 2, last - 1), (last - 1, last)]
        for n, unit in enumerate(rest):
            second_layer(unit[0], unit[1], free_banks[n], eng[CFG["yc"][len(CFG["yc"]) - len(rest) + n]])

        terms = []
        for t0, t1 in OUT_CHUNKS:
            pair = [keep.tile([P, t1 - t0], F32, name=f"term{j}_{t0}") for j in range(2)]
            terms.append(pair)

        def fetch(chunk, j):
            t0, t1 = OUT_CHUNKS[chunk]
            nc.vector.tensor_tensor(
                terms[chunk][j][:], y[:].indirect(pos_t[j][:, t0 // 16 : t1 // 16]), gate_t[j][:, t0:t1], ALU.mult
            )

        def finish(chunk):
            t0, t1 = OUT_CHUNKS[chunk]
            total = keep.tile([P, t1 - t0], F32, name=f"total{t0}")
            nc.vector.tensor_tensor(total[:], terms[chunk][0][:], terms[chunk][1][:], ALU.add)
            nc.sync.dma_start(out=out[:, t0:t1], in_=total[:])

        for chunk in range(len(OUT_CHUNKS)):
            fetch(chunk, 0)
            if chunk > 0:
                finish(chunk - 1)
            fetch(chunk, 1)
        finish(len(OUT_CHUNKS) - 1)
